import numpy as np
import ml_dtypes


def mxq(x, axis, fmt="e4m3"):
    dtype, down = {"e4m3": (ml_dtypes.float8_e4m3fn, 7), "e5m2": (ml_dtypes.float8_e5m2, 14)}[fmt]
    v = np.moveaxis(np.asarray(x, np.float32).astype(ml_dtypes.bfloat16).astype(np.float64), axis, -1)
    blocks = v.reshape(v.shape[:-1] + (-1, 32))
    amax = np.abs(blocks).max(-1, keepdims=True)
    byte = np.maximum(np.where(amax > 0, np.frexp(amax)[1] - 1 + 127, 0) - down, 1)
    scale = np.exp2(byte - 127.0)
    codes = (blocks / scale).astype(np.float32).astype(dtype).astype(np.float64)
    return np.moveaxis((codes * scale).reshape(v.shape), -1, axis)


WIDE = False


def mx_kscale(k):
    if not WIDE:
        return np.ones(k)
    levels = np.array([10, -10, 5, -5, 0])
    if k % 512:
        return np.exp2(np.random.permutation(np.resize(levels, k // 32))).repeat(32)
    a = np.empty((k // 512, 16))
    for p in range(k // 512):
        a[p, :8] = np.random.permutation(np.resize(levels, 8))
        for g in range(8):
            far = levels[np.abs(levels - a[p, g]) >= 10]
            a[p, g + 8] = far[np.random.randint(len(far))]
    return np.exp2(a.ravel()).repeat(32)


def f64(x):
    return np.asarray(x).astype(np.float64)


def striped(idx):
    return np.tile(idx.reshape(-1, 16).T, (8, 1)).astype(np.uint16)


def unstriped(offs):
    return offs[:16].T.reshape(-1).astype(np.int64)


E2M1 = np.array([0.0, 0.5, 1.0, 1.5, 2.0, 3.0, 4.0, 6.0, -0.0, -0.5, -1.0, -1.5, -2.0, -3.0, -4.0, -6.0])


def pack_weight(w, fmt):
    k, n = w.shape
    w = f64(np.asarray(w, np.float32).astype(ml_dtypes.bfloat16)).reshape(k // 32, 32, n)
    amax = np.abs(w).max(1)
    if fmt == "e4m3":
        byte = np.frexp(amax)[1] - 1 + 127 - 7
    else:
        mant, ex = np.frexp(amax / 6.0)
        byte = np.where(mant > 0.5, ex, ex - 1) + 127
    byte = np.clip(np.where(amax > 0, byte, 1), 1, 254)
    scaled = (w * np.exp2(127.0 - byte)[:, None, :]).reshape(k, n).astype(np.float32)
    by_word = np.ascontiguousarray(scaled.reshape(k // 512, 128, 4, n).transpose(0, 1, 3, 2))
    if fmt == "e4m3":
        words = by_word.astype(ml_dtypes.float8_e4m3fn).view(np.uint8)
    else:
        c = by_word.astype(ml_dtypes.float4_e2m1fn).view(np.uint8) & 0xF
        words = (c[..., 0::2] | (c[..., 1::2] << 4)).reshape(k // 512, 128, 2 * n)
    return np.ascontiguousarray(words), np.ascontiguousarray(byte.astype(np.uint8).reshape(k // 512, 16, n))


def unpack_weight(words, scales, fmt):
    g, _, n = scales.shape
    words = np.ascontiguousarray(words).reshape(g, 128, n, -1)
    if fmt == "e4m3":
        vals = words.view(ml_dtypes.float8_e4m3fn).astype(np.float64)
    else:
        nib = np.empty((g, 128, n, 4), np.uint8)
        nib[..., 0::2] = words & 0xF
        nib[..., 1::2] = words >> 4
        vals = E2M1[nib]
    vals = vals * np.repeat(np.exp2(scales.astype(np.float64) - 127.0), 8, axis=1)[..., None]
    return vals.transpose(0, 1, 3, 2).reshape(g * 512, n)


def gelu(v):
    return 0.5 * v * (1.0 + np.tanh(np.sqrt(2.0 / np.pi) * (v + 0.044715 * v**3)))


K, T, S, P, H, N = 1024, 2048, 1024, 512, 1024, 512

def setup_inputs():
    n = np.random.standard_normal
    s = mx_kscale(K)[:, None]
    u = mx_kscale(H)[:, None]
    tab_words, tab_scales = pack_weight(n((K, T)) * s, "e4m3")
    w2_words, w2_scales = pack_weight(0.45 * n((K, H)) / np.sqrt(K) / s, "e2m1")
    w3_words, w3_scales = pack_weight(2.0 * n((H, N)) / np.sqrt(H) / u, "e4m3")
    return {
        "tab_words": tab_words, "tab_scales": tab_scales,
        "offs": striped(np.random.permutation(T)[:S]),
        "pos1": striped(np.random.permutation(S)[:P]),
        "pos2": striped(np.random.permutation(S)[:P]),
        "w1": (1.3 * n((K, H)) / np.sqrt(K) / s).astype(np.float32),
        "w2_words": w2_words, "w2_scales": w2_scales,
        "temp": np.random.uniform(0.4, 1.6, H).astype(np.float32),
        "shift": (0.5 * n(H)).astype(np.float32),
        "lean": (np.where(n(H) < 0, -0.06, 0.25) * np.random.uniform(0.6, 1.4, H)).astype(np.float32),
        "gain": (np.random.uniform(2.0, 5.0, H) * u[:, 0]).astype(np.float32),
        "w3_words": w3_words, "w3_scales": w3_scales,
    }

def reference(tab_words, tab_scales, offs, pos1, pos2, w1, w2_words, w2_scales,
              temp, shift, lean, gain, w3_words, w3_scales):
    v = unpack_weight(tab_words, tab_scales, "e4m3")[:, unstriped(offs)]
    w2 = unpack_weight(w2_words, w2_scales, "e2m1")
    w3 = unpack_weight(w3_words, w3_scales, "e4m3")
    h = np.tanh(mxq(f64(w1), 0, "e4m3").T @ v) + (w2.T @ v)
    a = np.exp(f64(temp)[:, None] * h[:, unstriped(pos1)] + f64(shift)[:, None])
    top = h.max(axis=1)
    c = np.exp(h[:, unstriped(pos2)] - top[:, None])
    y = f64(gain)[:, None] * np.minimum(f64(lean)[:, None] * a, c)
    return np.tanh(w3.T @ mxq(y, 0, "e4m3"))

@@ -1,0 +1,277 @@
+from contextlib import ExitStack
+
+import concourse.mybir as mybir
+
+K, T, S, M, H, N = 1024, 2048, 1024, 512, 1024, 512
+FLOPS = 2 * (2 * K * H * S + H * N * M)
+
+F32 = mybir.dt.float32
+BF16 = mybir.dt.bfloat16
+I32 = mybir.dt.int32
+U32 = mybir.dt.uint32
+U16 = mybir.dt.uint16
+U8 = mybir.dt.uint8
+FP8X4 = mybir.dt.float8_e4m3fn_x4
+FP4X4 = mybir.dt.float4_e2m1fn_x4
+ACT = mybir.ActivationFunctionType
+ALU = mybir.AluOpType
+AXIS = mybir.AxisListType
+
+P = 128
+PACK = 4
+PASS = P * PACK
+BANK = 512
+HALF = M // 2
+
+
+def tile_list_tilt_bench_readings_kernel(
+    tc, tab_words, tab_scales, offs, pos1, pos2, w1, w2_words, w2_scales,
+    temp, shift, lean, gain, w3_words, w3_scales, out,
+):
+    nc = tc.nc
+    with ExitStack() as ctx:
+        keep = ctx.enter_context(tc.tile_pool(name="keep", bufs=1))
+        ring = ctx.enter_context(tc.tile_pool(name="ring", bufs=3))
+        psum = ctx.enter_context(tc.psum_pool(name="psum", bufs=8))
+
+        offs_sb = keep.tile([P, S // 16], U16, name="offs_sb")
+        pos1_sb = keep.tile([P, M // 16], U16, name="pos1_sb")
+        pos2_sb = keep.tile([P, M // 16], U16, name="pos2_sb")
+
+        tab_sc = keep.tile([P, T], U8, name="tab_sc", align_bytes=64)
+        w2_sc_raw = keep.tile([P, 2 * H], U8, name="w2_sc_raw", align_bytes=64)
+        w3_sc = keep.tile([P, 2 * N], U8, name="w3_sc", align_bytes=64)
+        v_sc1 = keep.tile([P, S], U8, name="v_sc1", align_bytes=64)
+        nc.vector.memset(tab_sc[:].bitcast(I32), 0)
+        nc.vector.memset(w2_sc_raw[:].bitcast(I32), 0)
+        nc.vector.memset(v_sc1[:].bitcast(I32), 0)
+        nc.vector.memset(w3_sc[:].bitcast(I32), 0)
+
+        w1_raw, tab_w, rows = {}, {}, {}
+
+        def load_w1(a, b):
+            w1_raw[a, b] = keep.tile([P, PACK, PASS], F32, name="w1_raw_%d_%d" % (a, b))
+            nc.sync.dma_start(
+                w1_raw[a, b][:],
+                w1[a * PASS : (a + 1) * PASS, b * PASS : (b + 1) * PASS].rearrange("(p j) c -> p j c", j=PACK),
+            )
+
+        def load_table(a):
+            tab_w[a] = keep.tile([P, T], U32, name="tab_w_%d" % a, align_bytes=64)
+            nc.sync.dma_start(tab_w[a][:].bitcast(I32), tab_words[a].rearrange("p t i -> p (t i)").bitcast(I32))
+
+        def load_row(key, vec):
+            rows[key] = keep.tile([P, 2 * PACK], F32, name="row_" + key)
+            nc.sync.dma_start(
+                rows[key][:].rearrange("p (b t) -> p b t", b=2),
+                vec.rearrange("(b p t) -> p b t", b=2, t=PACK),
+            )
+
+        nc.sync.dma_start(offs_sb[:], offs)
+        w2_raw = keep.tile([P, 2 * H], U16, name="w2_raw", align_bytes=64)
+        nc.sync.dma_start(
+            w2_raw[:].bitcast(I32).rearrange("p (a e) -> p a e", a=2),
+            w2_words.bitcast(I32).rearrange("a p e -> p a e"),
+        )
+        nc.sync.dma_start(pos1_sb[:], pos1)
+        for q in range(4):
+            nc.sync.dma_start(
+                tab_sc[32 * q : 32 * q + 8, :].bitcast(I32),
+                tab_scales[:, 4 * q : 4 * q + 4, :].bitcast(I32),
+            )
+        load_table(0)
+        load_w1(0, 0)
+        for q in range(4):
+            nc.sync.dma_start(
+                w2_sc_raw[32 * q : 32 * q + 4, :].bitcast(I32).rearrange("r (a e) -> r a e", a=2),
+                w2_scales[:, 4 * q : 4 * q + 4, :].bitcast(I32).rearrange("a r e -> r a e"),
+            )
+
+        load_w1(1, 0)
+        load_table(1)
+        nc.sync.dma_start(pos2_sb[:], pos2)
+        load_row("temp", temp)
+        load_row("shift", shift)
+
+        v_sc = keep.tile([P, S], U8, name="v_sc", align_bytes=64)
+        nc.vector.tensor_copy(v_sc[:], tab_sc[:].indirect(offs_sb[:]))
+        nc.sync.dma_start(v_sc1[0:112, :].bitcast(I32), v_sc[4:116, :].bitcast(I32))
+
+        load_row("lean", lean)
+        load_row("gain", gain)
+        load_w1(0, 1)
+        load_w1(1, 1)
+        w3_w = keep.tile([P, 2 * N], U32, name="w3_w", align_bytes=64)
+        nc.sync.dma_start(
+            w3_w[:].bitcast(I32).rearrange("p (a e) -> p a e", a=2),
+            w3_words.rearrange("a p e i -> p a (e i)").bitcast(I32),
+        )
+        for q in range(4):
+            nc.sync.dma_start(
+                w3_sc[32 * q : 32 * q + 4, :].bitcast(I32).rearrange("r (a e) -> r a e", a=2),
+                w3_scales[:, 4 * q : 4 * q + 4, :].bitcast(I32).rearrange("a r e -> r a e"),
+            )
+
+        w1_bf, w1_codes, w1_sc = {}, {}, {}
+
+        def round_w1(a, b, copy):
+            w1_bf[a, b] = keep.tile([P, PASS * PACK], BF16, name="w1_bf_%d_%d" % (a, b), align_bytes=64)
+            copy(
+                w1_bf[a, b][:].rearrange("p (t m j) -> p m j t", t=PACK, j=PACK),
+                w1_raw[a, b][:].rearrange("p j (m t) -> p m j t", t=PACK),
+            )
+
+            w1_codes[a, b] = keep.tile([P, PASS], U32, name="w1_codes_%d_%d" % (a, b), align_bytes=64)
+            w1_sc[a, b] = keep.tile([P, PASS], U8, name="w1_sc_%d_%d" % (a, b), align_bytes=64)
+
+        def quantize_w1(a, b, lo=0, hi=PASS):
+            nc.vector.quantize_mx(
+                out=w1_codes[a, b][:, lo:hi].bitcast(FP8X4), scales=w1_sc[a, b][:, lo:hi],
+                in_=w1_bf[a, b][:, PACK * lo : PACK * hi],
+            )
+
+        w2_w = keep.tile([P, 2 * H], U16, name="w2_w", align_bytes=64)
+        w2_sc = keep.tile([P, 2 * H], U8, name="w2_sc", align_bytes=64)
+
+        def deal(dealt, raw, copy):
+            copy(
+                dealt[:].rearrange("p (g t c i) -> p g c t i", t=PACK, c=32, i=4),
+                raw[:].rearrange("p (g c i t) -> p g c t i", t=PACK, c=32, i=4),
+            )
+
+        deal(w2_w, w2_raw, nc.scalar.copy)
+        round_w1(0, 0, nc.scalar.copy)
+        round_w1(1, 0, nc.scalar.copy)
+
+        v_w = {}
+
+        def gather_words(a, half):
+            v_w[a, half] = keep.tile([P, BANK], U32, name="v_w_%d_%d" % (a, half), align_bytes=64)
+            nc.vector.tensor_copy(v_w[a, half][:], tab_w[a][:].indirect(offs_sb[:, 32 * half : 32 * half + 32]))
+
+        gather_words(0, 0)
+        gather_words(0, 1)
+        deal(w2_sc, w2_sc_raw, nc.vector.tensor_copy)
+        quantize_w1(0, 0)
+        gather_words(1, 0)
+        quantize_w1(1, 0, 0, P)
+        gather_words(1, 1)
+        quantize_w1(1, 0, P, PASS)
+
+        h, neg_top = {}, {}
+        y_rows = [keep.tile([P, PACK, M], BF16, name="y_rows_%d" % b, align_bytes=64) for b in range(2)]
+        y_codes, y_sc = {}, {}
+
+        def first_stage(i):
+            b, t = divmod(i, PACK)
+            h[i] = ring.tile([P, S], F32, name="h")
+            bounded, linear = [], []
+            for half in range(2):
+                cols = slice(half * BANK, (half + 1) * BANK)
+                bounded.append(psum.tile([P, BANK], F32, name="acc"))
+                for a in range(2):
+                    nc.tensor.matmul_mx(
+                        out=bounded[half][:],
+                        lhsT=w1_codes[a, b][:, t * P : (t + 1) * P].bitcast(FP8X4),
+                        lhsT_scale=w1_sc[a, b][:, t * P : (t + 1) * P],
+                        rhs=v_w[a, half][:].bitcast(FP8X4),
+                        rhs_scale=v_sc[4 * a : P, cols],
+                        start=(a == 0), stop=(a == 1),
+                    )
+                linear.append(psum.tile([P, BANK], F32, name="acc"))
+                for a in range(2):
+                    wcols = slice(a * H + i * P, a * H + (i + 1) * P)
+                    nc.tensor.matmul_mx(
+                        out=linear[half][:],
+                        lhsT=w2_w[:, wcols].bitcast(FP4X4),
+                        lhsT_scale=w2_sc[:, wcols],
+                        rhs=v_w[a, half][:].bitcast(FP8X4),
+                        rhs_scale=(v_sc, v_sc1)[a][:, cols],
+                        start=(a == 0), stop=(a == 1),
+                    )
+            for half in range(2):
+                cols = slice(half * BANK, (half + 1) * BANK)
+                nc.scalar.activation(out=h[i][:, cols], in_=bounded[half][:], func=ACT.Tanh)
+                nc.vector.tensor_tensor(out=h[i][:, cols], in0=h[i][:, cols], in1=linear[half][:], op=ALU.add)
+            neg_top[i] = ring.tile([P, 1], F32, name="neg_top")
+            nc.vector.tensor_reduce(out=neg_top[i][:], in_=h[i][:], axis=AXIS.X, op=ALU.max, negate=True)
+
+        def look(i, lo, hi):
+            b, t = divmod(i, PACK)
+            lists = slice(lo // 16, hi // 16)
+            nudged = ring.tile([P, hi - lo], F32, name="nudged")
+            quiet = ring.tile([P, hi - lo], F32, name="quiet")
+            nc.scalar.activation(
+                out=nudged[:], in_=h[i][:].indirect(pos1_sb[:, lists]), func=ACT.Exp,
+                bias=rows["shift"][:, i : i + 1], scale=rows["temp"][:, i : i + 1],
+            )
+            nc.scalar.activation(
+                out=quiet[:], in_=h[i][:].indirect(pos2_sb[:, lists]), func=ACT.Exp, bias=neg_top[i][:],
+            )
+            lesser = ring.tile([P, hi - lo], F32, name="lesser")
+            nc.vector.scalar_tensor_tensor(
+                out=lesser[:], in0=nudged[:], scalar=rows["lean"][:, i : i + 1], in1=quiet[:],
+                op0=ALU.mult, op1=ALU.min,
+            )
+            nc.vector.tensor_scalar(
+                out=y_rows[b][:, t, lo:hi], in0=lesser[:], scalar1=rows["gain"][:, i : i + 1], scalar2=None,
+                op0=ALU.mult,
+            )
+
+        def quantize_y(b, half):
+            woven = ring.tile([P, HALF * PACK], BF16, name="woven", align_bytes=64)
+            nc.vector.tensor_copy(
+                woven[:].rearrange("p (c i t) -> p c t i", i=4, t=PACK),
+                y_rows[b][:, :, half * HALF : (half + 1) * HALF].rearrange("p t (c i) -> p c t i", i=4),
+            )
+            y_codes[b, half] = keep.tile([P, HALF], U32, name="y_codes_%d_%d" % (b, half), align_bytes=64)
+            y_sc[b, half] = keep.tile([P, HALF], U8, name="y_sc_%d_%d" % (b, half), align_bytes=64)
+            nc.vector.quantize_mx(out=y_codes[b, half][:].bitcast(FP8X4), scales=y_sc[b, half][:], in_=woven[:])
+
+        scores = {}
+
+        def second_stage(b, half):
+            for pair in range(2):
+                if b == 0:
+                    scores[half, pair] = psum.tile([P, BANK], F32, name="acc")
+                for u in range(2):
+                    n0 = b * N + (2 * pair + u) * P
+                    nc.tensor.matmul_mx(
+                        out=scores[half, pair][:, u * HALF : (u + 1) * HALF],
+                        lhsT=w3_w[:, n0 : n0 + P].bitcast(FP8X4),
+                        lhsT_scale=w3_sc[:, n0 : n0 + P],
+                        rhs=y_codes[b, half][:].bitcast(FP8X4),
+                        rhs_scale=y_sc[b, half][:],
+                        start=(b == 0 and u == 0), stop=(b == 1 and u == 1),
+                    )
+
+        def finish(half):
+            for pair in range(2):
+                result = keep.tile([P, BANK], F32, name="result_%d_%d" % (half, pair))
+                nc.scalar.activation(out=result[:], in_=scores[half, pair][:], func=ACT.Tanh)
+                nc.sync.dma_start(
+                    out[2 * pair * P : (2 * pair + 2) * P, half * HALF : (half + 1) * HALF].rearrange("(u p) m -> p u m", u=2),
+                    result[:].rearrange("p (u m) -> p u m", u=2),
+                )
+
+        last = 2 * PACK - 1
+        first_stage(0)
+        for i in range(last):
+            first_stage(i + 1)
+            if i in (1, 2):
+                quantize_w1(i - 1, 1)
+            if i in (0, 1):
+                round_w1(i, 1, nc.vector.tensor_copy)
+            look(i, 0, M)
+            if i == PACK - 1:
+                quantize_y(0, 0)
+                quantize_y(0, 1)
+        second_stage(0, 0)
+        second_stage(0, 1)
+        for half in range(2):
+            look(last, half * HALF, (half + 1) * HALF)
+        for half in range(2):
+            quantize_y(1, half)
+            second_stage(1, half)
+        for half in range(2):
+            finish(half)

@@ -31,7 +31,7 @@ def tile_list_tilt_bench_readings_kernel(
     nc = tc.nc
     with ExitStack() as ctx:
         keep = ctx.enter_context(tc.tile_pool(name="keep", bufs=1))
-        ring = ctx.enter_context(tc.tile_pool(name="ring", bufs=3))
+        ring = ctx.enter_context(tc.tile_pool(name="ring", bufs=2))
         psum = ctx.enter_context(tc.psum_pool(name="psum", bufs=8))
 
         offs_sb = keep.tile([P, S // 16], U16, name="offs_sb")
@@ -86,20 +86,27 @@ def tile_list_tilt_bench_readings_kernel(
                 w2_sc_raw[32 * q : 32 * q + 4, :].bitcast(I32).rearrange("r (a e) -> r a e", a=2),
                 w2_scales[:, 4 * q : 4 * q + 4, :].bitcast(I32).rearrange("a r e -> r a e"),
             )
-
         load_w1(1, 0)
         load_table(1)
-        nc.sync.dma_start(pos2_sb[:], pos2)
-        load_row("temp", temp)
-        load_row("shift", shift)
+
+        v_w = {}
+
+        def gather_words(a, half):
+            v_w[a, half] = keep.tile([P, BANK], U32, name="v_w_%d_%d" % (a, half), align_bytes=64)
+            nc.vector.tensor_copy(v_w[a, half][:], tab_w[a][:].indirect(offs_sb[:, 32 * half : 32 * half + 32]))
 
         v_sc = keep.tile([P, S], U8, name="v_sc", align_bytes=64)
         nc.vector.tensor_copy(v_sc[:], tab_sc[:].indirect(offs_sb[:]))
+        gather_words(0, 0)
+        gather_words(0, 1)
         nc.sync.dma_start(v_sc1[0:112, :].bitcast(I32), v_sc[4:116, :].bitcast(I32))
 
+        load_row("temp", temp)
+        load_row("shift", shift)
+        nc.sync.dma_start(pos2_sb[:], pos2)
+        load_w1(0, 1)
         load_row("lean", lean)
         load_row("gain", gain)
-        load_w1(0, 1)
         load_w1(1, 1)
         w3_w = keep.tile([P, 2 * N], U32, name="w3_w", align_bytes=64)
         nc.sync.dma_start(
@@ -114,15 +121,17 @@ def tile_list_tilt_bench_readings_kernel(
 
         w1_bf, w1_codes, w1_sc = {}, {}, {}
 
-        def round_w1(a, b, copy):
-            w1_bf[a, b] = keep.tile([P, PASS * PACK], BF16, name="w1_bf_%d_%d" % (a, b), align_bytes=64)
-            copy(
-                w1_bf[a, b][:].rearrange("p (t m j) -> p m j t", t=PACK, j=PACK),
-                w1_raw[a, b][:].rearrange("p j (m t) -> p m j t", t=PACK),
-            )
+        for a in range(2):
+            for b in range(2):
+                w1_bf[a, b] = keep.tile([P, PASS * PACK], BF16, name="w1_bf_%d_%d" % (a, b), align_bytes=64)
+                w1_codes[a, b] = keep.tile([P, PASS], U32, name="w1_codes_%d_%d" % (a, b), align_bytes=64)
+                w1_sc[a, b] = keep.tile([P, PASS], U8, name="w1_sc_%d_%d" % (a, b), align_bytes=64)
 
-            w1_codes[a, b] = keep.tile([P, PASS], U32, name="w1_codes_%d_%d" % (a, b), align_bytes=64)
-            w1_sc[a, b] = keep.tile([P, PASS], U8, name="w1_sc_%d_%d" % (a, b), align_bytes=64)
+        def round_w1(a, b, copy, lo=0, hi=P):
+            copy(
+                w1_bf[a, b][:].rearrange("p (t m j) -> p m t j", t=PACK, j=PACK)[:, lo:hi, :, :],
+                w1_raw[a, b][:].rearrange("p j (m t) -> p m t j", t=PACK)[:, lo:hi, :, :],
+            )
 
         def quantize_w1(a, b, lo=0, hi=PASS):
             nc.vector.quantize_mx(
@@ -142,15 +151,6 @@ def tile_list_tilt_bench_readings_kernel(
         deal(w2_w, w2_raw, nc.scalar.copy)
         round_w1(0, 0, nc.scalar.copy)
         round_w1(1, 0, nc.scalar.copy)
-
-        v_w = {}
-
-        def gather_words(a, half):
-            v_w[a, half] = keep.tile([P, BANK], U32, name="v_w_%d_%d" % (a, half), align_bytes=64)
-            nc.vector.tensor_copy(v_w[a, half][:], tab_w[a][:].indirect(offs_sb[:, 32 * half : 32 * half + 32]))
-
-        gather_words(0, 0)
-        gather_words(0, 1)
         deal(w2_sc, w2_sc_raw, nc.vector.tensor_copy)
         quantize_w1(0, 0)
         gather_words(1, 0)
@@ -158,79 +158,86 @@ def tile_list_tilt_bench_readings_kernel(
         gather_words(1, 1)
         quantize_w1(1, 0, P, PASS)
 
-        h, neg_top = {}, {}
-        y_rows = [keep.tile([P, PACK, M], BF16, name="y_rows_%d" % b, align_bytes=64) for b in range(2)]
-        y_codes, y_sc = {}, {}
+        h, neg_top, bounded, linear, nudged, quiet, lesser = {}, {}, {}, {}, {}, {}, {}
+        last = 2 * PACK - 1
+        woven = [keep.tile([P, M * PACK], BF16, name="woven_%d" % b, align_bytes=64) for b in range(2)]
+        y_codes, y_sc, scores = {}, {}, {}
 
-        def first_stage(i):
+        def products(i):
             b, t = divmod(i, PACK)
             h[i] = ring.tile([P, S], F32, name="h")
-            bounded, linear = [], []
             for half in range(2):
-                cols = slice(half * BANK, (half + 1) * BANK)
-                bounded.append(psum.tile([P, BANK], F32, name="acc"))
-                for a in range(2):
+                bounded[i, half] = psum.tile([P, BANK], F32, name="acc")
+                linear[i, half] = psum.tile([P, BANK], F32, name="acc")
+            for a in range(2):
+                for half in range(2):
+                    cols = slice(half * BANK, (half + 1) * BANK)
+                    wcols = slice(a * H + i * P, a * H + (i + 1) * P)
                     nc.tensor.matmul_mx(
-                        out=bounded[half][:],
+                        out=bounded[i, half][:],
                         lhsT=w1_codes[a, b][:, t * P : (t + 1) * P].bitcast(FP8X4),
                         lhsT_scale=w1_sc[a, b][:, t * P : (t + 1) * P],
                         rhs=v_w[a, half][:].bitcast(FP8X4),
                         rhs_scale=v_sc[4 * a : P, cols],
                         start=(a == 0), stop=(a == 1),
                     )
-                linear.append(psum.tile([P, BANK], F32, name="acc"))
-                for a in range(2):
-                    wcols = slice(a * H + i * P, a * H + (i + 1) * P)
                     nc.tensor.matmul_mx(
-                        out=linear[half][:],
+                        out=linear[i, half][:],
                         lhsT=w2_w[:, wcols].bitcast(FP4X4),
                         lhsT_scale=w2_sc[:, wcols],
                         rhs=v_w[a, half][:].bitcast(FP8X4),
                         rhs_scale=(v_sc, v_sc1)[a][:, cols],
                         start=(a == 0), stop=(a == 1),
                     )
-            for half in range(2):
-                cols = slice(half * BANK, (half + 1) * BANK)
-                nc.scalar.activation(out=h[i][:, cols], in_=bounded[half][:], func=ACT.Tanh)
-                nc.vector.tensor_tensor(out=h[i][:, cols], in0=h[i][:, cols], in1=linear[half][:], op=ALU.add)
+
+        def bound(i, half):
+            nc.scalar.activation(out=h[i][:, half * BANK : (half + 1) * BANK], in_=bounded[i, half][:], func=ACT.Tanh)
+
+        def add_linear(i, half):
+            cols = slice(half * BANK, (half + 1) * BANK)
+            nc.vector.tensor_tensor(out=h[i][:, cols], in0=h[i][:, cols], in1=linear[i, half][:], op=ALU.add)
+
+        def row_top(i):
             neg_top[i] = ring.tile([P, 1], F32, name="neg_top")
             nc.vector.tensor_reduce(out=neg_top[i][:], in_=h[i][:], axis=AXIS.X, op=ALU.max, negate=True)
 
         def look(i, lo, hi):
-            b, t = divmod(i, PACK)
             lists = slice(lo // 16, hi // 16)
-            nudged = ring.tile([P, hi - lo], F32, name="nudged")
-            quiet = ring.tile([P, hi - lo], F32, name="quiet")
+            nudged[i, lo] = ring.tile([P, hi - lo], F32, name="nudged")
+            quiet[i, lo] = ring.tile([P, hi - lo], F32, name="quiet")
             nc.scalar.activation(
-                out=nudged[:], in_=h[i][:].indirect(pos1_sb[:, lists]), func=ACT.Exp,
+                out=nudged[i, lo][:], in_=h[i][:].indirect(pos1_sb[:, lists]), func=ACT.Exp,
                 bias=rows["shift"][:, i : i + 1], scale=rows["temp"][:, i : i + 1],
             )
             nc.scalar.activation(
-                out=quiet[:], in_=h[i][:].indirect(pos2_sb[:, lists]), func=ACT.Exp, bias=neg_top[i][:],
+                out=quiet[i, lo][:], in_=h[i][:].indirect(pos2_sb[:, lists]), func=ACT.Exp, bias=neg_top[i][:],
             )
-            lesser = ring.tile([P, hi - lo], F32, name="lesser")
+
+        def take_lesser(i, lo, hi):
+            lesser[i, lo] = ring.tile([P, hi - lo], F32, name="lesser")
             nc.vector.scalar_tensor_tensor(
-                out=lesser[:], in0=nudged[:], scalar=rows["lean"][:, i : i + 1], in1=quiet[:],
+                out=lesser[i, lo][:], in0=nudged[i, lo][:], scalar=rows["lean"][:, i : i + 1], in1=quiet[i, lo][:],
                 op0=ALU.mult, op1=ALU.min,
             )
+
+        def weave(i, lo, hi):
+            b, t = divmod(i, PACK)
             nc.vector.tensor_scalar(
-                out=y_rows[b][:, t, lo:hi], in0=lesser[:], scalar1=rows["gain"][:, i : i + 1], scalar2=None,
-                op0=ALU.mult,
+                out=woven[b][:, PACK * lo : PACK * hi].rearrange("p (m t) -> p t m", t=PACK)[:, t, :],
+                in0=lesser[i, lo][:], scalar1=rows["gain"][:, i : i + 1], scalar2=None, op0=ALU.mult,
             )
 
-        def quantize_y(b, half):
-            woven = ring.tile([P, HALF * PACK], BF16, name="woven", align_bytes=64)
-            nc.vector.tensor_copy(
-                woven[:].rearrange("p (c i t) -> p c t i", i=4, t=PACK),
-                y_rows[b][:, :, half * HALF : (half + 1) * HALF].rearrange("p t (c i) -> p c t i", i=4),
+        def quantize_y(b, lo, hi):
+            nc.vector.quantize_mx(
+                out=y_codes[b][:, lo:hi].bitcast(FP8X4), scales=y_sc[b][:, lo:hi], in_=woven[b][:, PACK * lo : PACK * hi],
             )
-            y_codes[b, half] = keep.tile([P, HALF], U32, name="y_codes_%d_%d" % (b, half), align_bytes=64)
-            y_sc[b, half] = keep.tile([P, HALF], U8, name="y_sc_%d_%d" % (b, half), align_bytes=64)
-            nc.vector.quantize_mx(out=y_codes[b, half][:].bitcast(FP8X4), scales=y_sc[b, half][:], in_=woven[:])
 
-        scores = {}
+        for b in range(2):
+            y_codes[b] = keep.tile([P, M], U32, name="y_codes_%d" % b, align_bytes=64)
+            y_sc[b] = keep.tile([P, M], U8, name="y_sc_%d" % b, align_bytes=64)
 
         def second_stage(b, half):
+            cols = slice(half * HALF, (half + 1) * HALF)
             for pair in range(2):
                 if b == 0:
                     scores[half, pair] = psum.tile([P, BANK], F32, name="acc")
@@ -240,8 +247,8 @@ def tile_list_tilt_bench_readings_kernel(
                         out=scores[half, pair][:, u * HALF : (u + 1) * HALF],
                         lhsT=w3_w[:, n0 : n0 + P].bitcast(FP8X4),
                         lhsT_scale=w3_sc[:, n0 : n0 + P],
-                        rhs=y_codes[b, half][:].bitcast(FP8X4),
-                        rhs_scale=y_sc[b, half][:],
+                        rhs=y_codes[b][:, cols].bitcast(FP8X4),
+                        rhs_scale=y_sc[b][:, cols],
                         start=(b == 0 and u == 0), stop=(b == 1 and u == 1),
                     )
 
@@ -249,29 +256,49 @@ def tile_list_tilt_bench_readings_kernel(
             for pair in range(2):
                 result = keep.tile([P, BANK], F32, name="result_%d_%d" % (half, pair))
                 nc.scalar.activation(out=result[:], in_=scores[half, pair][:], func=ACT.Tanh)
-                nc.sync.dma_start(
+                (nc.scalar if half + pair == 2 else nc.sync).dma_start(
                     out[2 * pair * P : (2 * pair + 2) * P, half * HALF : (half + 1) * HALF].rearrange("(u p) m -> p u m", u=2),
                     result[:].rearrange("p (u m) -> p u m", u=2),
                 )
 
-        last = 2 * PACK - 1
-        first_stage(0)
+        products(0)
+        for half in range(2):
+            bound(0, half)
+            add_linear(0, half)
+        row_top(0)
         for i in range(last):
-            first_stage(i + 1)
+            products(i + 1)
+            bound(i + 1, 0)
+            if i > 0:
+                take_lesser(i - 1, 0, M)
+            add_linear(i + 1, 0)
+            bound(i + 1, 1)
+            if i > 0:
+                weave(i - 1, 0, M)
+            add_linear(i + 1, 1)
+            if i == 0:
+                round_w1(0, 1, nc.vector.tensor_copy)
             if i in (1, 2):
                 quantize_w1(i - 1, 1)
-            if i in (0, 1):
-                round_w1(i, 1, nc.vector.tensor_copy)
+            if i == PACK:
+                quantize_y(0, 0, M)
+            row_top(i + 1)
             look(i, 0, M)
-            if i == PACK - 1:
-                quantize_y(0, 0)
-                quantize_y(0, 1)
+            if i in (0, 1):
+                round_w1(1, 1, nc.scalar.copy, i * P // 2, (i + 1) * P // 2)
         second_stage(0, 0)
         second_stage(0, 1)
+        take_lesser(last - 1, 0, M)
+        weave(last - 1, 0, M)
+        look(last, 0, HALF)
+        look(last, HALF, M)
+        take_lesser(last, 0, HALF)
+        weave(last, 0, HALF)
+        take_lesser(last, HALF, M)
+        quantize_y(1, 0, HALF)
+        weave(last, HALF, M)
+        quantize_y(1, HALF, M)
         for half in range(2):
-            look(last, half * HALF, (half + 1) * HALF)
-        for half in range(2):
-            quantize_y(1, half)
             second_stage(1, half)
         for half in range(2):
             finish(half)

@@ -160,6 +160,7 @@ def tile_list_tilt_bench_readings_kernel(
 
         h, neg_top, bounded, linear, nudged, quiet, lesser = {}, {}, {}, {}, {}, {}, {}
         last = 2 * PACK - 1
+        y_rows = [keep.tile([P, PACK, M], BF16, name="y_rows_%d" % b, align_bytes=64) for b in range(2)]
         woven = [keep.tile([P, M * PACK], BF16, name="woven_%d" % b, align_bytes=64) for b in range(2)]
         y_codes, y_sc, scores = {}, {}, {}
 
@@ -220,11 +221,17 @@ def tile_list_tilt_bench_readings_kernel(
                 op0=ALU.mult, op1=ALU.min,
             )
 
-        def weave(i, lo, hi):
+        def apply_gain(i, lo, hi):
             b, t = divmod(i, PACK)
             nc.vector.tensor_scalar(
-                out=woven[b][:, PACK * lo : PACK * hi].rearrange("p (m t) -> p t m", t=PACK)[:, t, :],
-                in0=lesser[i, lo][:], scalar1=rows["gain"][:, i : i + 1], scalar2=None, op0=ALU.mult,
+                out=y_rows[b][:, t, lo:hi], in0=lesser[i, lo][:], scalar1=rows["gain"][:, i : i + 1], scalar2=None,
+                op0=ALU.mult,
+            )
+
+        def weave(b, lo, hi):
+            nc.vector.tensor_copy(
+                woven[b][:, PACK * lo : PACK * hi].rearrange("p (c i t) -> p c t i", i=4, t=PACK),
+                y_rows[b][:, :, lo:hi].rearrange("p t (c i) -> p c t i", i=4),
             )
 
         def quantize_y(b, lo, hi):
@@ -268,35 +275,36 @@ def tile_list_tilt_bench_readings_kernel(
         row_top(0)
         for i in range(last):
             products(i + 1)
-            bound(i + 1, 0)
             if i > 0:
                 take_lesser(i - 1, 0, M)
-            add_linear(i + 1, 0)
-            bound(i + 1, 1)
+            for half in range(2):
+                bound(i + 1, half)
+                add_linear(i + 1, half)
             if i > 0:
-                weave(i - 1, 0, M)
-            add_linear(i + 1, 1)
-            if i == 0:
-                round_w1(0, 1, nc.vector.tensor_copy)
-            if i in (1, 2):
-                quantize_w1(i - 1, 1)
-            if i == PACK:
-                quantize_y(0, 0, M)
+                apply_gain(i - 1, 0, M)
             row_top(i + 1)
             look(i, 0, M)
+            if i in (1, 2):
+                quantize_w1(i - 1, 1)
             if i in (0, 1):
-                round_w1(1, 1, nc.scalar.copy, i * P // 2, (i + 1) * P // 2)
+                round_w1(i, 1, nc.vector.tensor_copy)
+            if i == PACK:
+                weave(0, 0, M)
+            if i == PACK + 1:
+                quantize_y(0, 0, M)
         second_stage(0, 0)
         second_stage(0, 1)
         take_lesser(last - 1, 0, M)
-        weave(last - 1, 0, M)
+        apply_gain(last - 1, 0, M)
         look(last, 0, HALF)
         look(last, HALF, M)
         take_lesser(last, 0, HALF)
-        weave(last, 0, HALF)
+        apply_gain(last, 0, HALF)
+        weave(1, 0, HALF)
         take_lesser(last, HALF, M)
         quantize_y(1, 0, HALF)
-        weave(last, HALF, M)
+        apply_gain(last, HALF, M)
+        weave(1, HALF, M)
         quantize_y(1, HALF, M)
         for half in range(2):
             second_stage(1, half)

from contextlib import ExitStack

import concourse.mybir as mybir

K, T, S, M, H, N = 1024, 2048, 1024, 512, 1024, 512
FLOPS = 2 * (2 * K * H * S + H * N * M)

F32 = mybir.dt.float32
BF16 = mybir.dt.bfloat16
I32 = mybir.dt.int32
U32 = mybir.dt.uint32
U16 = mybir.dt.uint16
U8 = mybir.dt.uint8
FP8X4 = mybir.dt.float8_e4m3fn_x4
FP4X4 = mybir.dt.float4_e2m1fn_x4
ACT = mybir.ActivationFunctionType
ALU = mybir.AluOpType
AXIS = mybir.AxisListType

P = 128
PACK = 4
PASS = P * PACK
BANK = 512
HALF = M // 2


def tile_list_tilt_bench_readings_kernel(
    tc, tab_words, tab_scales, offs, pos1, pos2, w1, w2_words, w2_scales,
    temp, shift, lean, gain, w3_words, w3_scales, out,
):
    nc = tc.nc
    with ExitStack() as ctx:
        keep = ctx.enter_context(tc.tile_pool(name="keep", bufs=1))
        ring = ctx.enter_context(tc.tile_pool(name="ring", bufs=2))
        psum = ctx.enter_context(tc.psum_pool(name="psum", bufs=8))

        offs_sb = keep.tile([P, S // 16], U16, name="offs_sb")
        pos1_sb = keep.tile([P, M // 16], U16, name="pos1_sb")
        pos2_sb = keep.tile([P, M // 16], U16, name="pos2_sb")

        tab_sc = keep.tile([P, T], U8, name="tab_sc", align_bytes=64)
        w2_sc_raw = keep.tile([P, 2 * H], U8, name="w2_sc_raw", align_bytes=64)
        w3_sc = keep.tile([P, 2 * N], U8, name="w3_sc", align_bytes=64)
        v_sc1 = keep.tile([P, S], U8, name="v_sc1", align_bytes=64)
        nc.vector.memset(tab_sc[:].bitcast(I32), 0)
        nc.vector.memset(w2_sc_raw[:].bitcast(I32), 0)
        nc.vector.memset(v_sc1[:].bitcast(I32), 0)
        nc.vector.memset(w3_sc[:].bitcast(I32), 0)

        w1_raw, tab_w, rows = {}, {}, {}

        def load_w1(a, b):
            w1_raw[a, b] = keep.tile([P, PACK, PASS], F32, name="w1_raw_%d_%d" % (a, b))
            nc.sync.dma_start(
                w1_raw[a, b][:],
                w1[a * PASS : (a + 1) * PASS, b * PASS : (b + 1) * PASS].rearrange("(p j) c -> p j c", j=PACK),
            )

        def load_table(a):
            tab_w[a] = keep.tile([P, T], U32, name="tab_w_%d" % a, align_bytes=64)
            nc.sync.dma_start(tab_w[a][:].bitcast(I32), tab_words[a].rearrange("p t i -> p (t i)").bitcast(I32))

        def load_row(key, vec):
            rows[key] = keep.tile([P, 2 * PACK], F32, name="row_" + key)
            nc.sync.dma_start(
                rows[key][:].rearrange("p (b t) -> p b t", b=2),
                vec.rearrange("(b p t) -> p b t", b=2, t=PACK),
            )

        nc.sync.dma_start(offs_sb[:], offs)
        w2_raw = keep.tile([P, 2 * H], U16, name="w2_raw", align_bytes=64)
        nc.sync.dma_start(
            w2_raw[:].bitcast(I32).rearrange("p (a e) -> p a e", a=2),
            w2_words.bitcast(I32).rearrange("a p e -> p a e"),
        )
        nc.sync.dma_start(pos1_sb[:], pos1)
        for q in range(4):
            nc.sync.dma_start(
                tab_sc[32 * q : 32 * q + 8, :].bitcast(I32),
                tab_scales[:, 4 * q : 4 * q + 4, :].bitcast(I32),
            )
        load_table(0)
        load_w1(0, 0)
        for q in range(4):
            nc.sync.dma_start(
                w2_sc_raw[32 * q : 32 * q + 4, :].bitcast(I32).rearrange("r (a e) -> r a e", a=2),
                w2_scales[:, 4 * q : 4 * q + 4, :].bitcast(I32).rearrange("a r e -> r a e"),
            )
        load_w1(1, 0)
        load_table(1)

        v_w = {}

        def gather_words(a, half):
            v_w[a, half] = keep.tile([P, BANK], U32, name="v_w_%d_%d" % (a, half), align_bytes=64)
            nc.vector.tensor_copy(v_w[a, half][:], tab_w[a][:].indirect(offs_sb[:, 32 * half : 32 * half + 32]))

        v_sc = keep.tile([P, S], U8, name="v_sc", align_bytes=64)
        nc.vector.tensor_copy(v_sc[:], tab_sc[:].indirect(offs_sb[:]))
        gather_words(0, 0)
        gather_words(0, 1)
        nc.sync.dma_start(v_sc1[0:112, :].bitcast(I32), v_sc[4:116, :].bitcast(I32))

        load_row("temp", temp)
        load_row("shift", shift)
        nc.sync.dma_start(pos2_sb[:], pos2)
        load_w1(0, 1)
        load_row("lean", lean)
        load_row("gain", gain)
        load_w1(1, 1)
        w3_w = keep.tile([P, 2 * N], U32, name="w3_w", align_bytes=64)
        nc.sync.dma_start(
            w3_w[:].bitcast(I32).rearrange("p (a e) -> p a e", a=2),
            w3_words.rearrange("a p e i -> p a (e i)").bitcast(I32),
        )
        for q in range(4):
            nc.sync.dma_start(
                w3_sc[32 * q : 32 * q + 4, :].bitcast(I32).rearrange("r (a e) -> r a e", a=2),
                w3_scales[:, 4 * q : 4 * q + 4, :].bitcast(I32).rearrange("a r e -> r a e"),
            )

        w1_bf, w1_codes, w1_sc = {}, {}, {}

        for a in range(2):
            for b in range(2):
                w1_bf[a, b] = keep.tile([P, PASS * PACK], BF16, name="w1_bf_%d_%d" % (a, b), align_bytes=64)
                w1_codes[a, b] = keep.tile([P, PASS], U32, name="w1_codes_%d_%d" % (a, b), align_bytes=64)
                w1_sc[a, b] = keep.tile([P, PASS], U8, name="w1_sc_%d_%d" % (a, b), align_bytes=64)

        def round_w1(a, b, copy, lo=0, hi=P):
            copy(
                w1_bf[a, b][:].rearrange("p (t m j) -> p m t j", t=PACK, j=PACK)[:, lo:hi, :, :],
                w1_raw[a, b][:].rearrange("p j (m t) -> p m t j", t=PACK)[:, lo:hi, :, :],
            )

        def quantize_w1(a, b, lo=0, hi=PASS):
            nc.vector.quantize_mx(
                out=w1_codes[a, b][:, lo:hi].bitcast(FP8X4), scales=w1_sc[a, b][:, lo:hi],
                in_=w1_bf[a, b][:, PACK * lo : PACK * hi],
            )

        w2_w = keep.tile([P, 2 * H], U16, name="w2_w", align_bytes=64)
        w2_sc = keep.tile([P, 2 * H], U8, name="w2_sc", align_bytes=64)

        def deal(dealt, raw, copy):
            copy(
                dealt[:].rearrange("p (g t c i) -> p g c t i", t=PACK, c=32, i=4),
                raw[:].rearrange("p (g c i t) -> p g c t i", t=PACK, c=32, i=4),
            )

        deal(w2_w, w2_raw, nc.scalar.copy)
        round_w1(0, 0, nc.scalar.copy)
        round_w1(1, 0, nc.scalar.copy)
        deal(w2_sc, w2_sc_raw, nc.vector.tensor_copy)
        quantize_w1(0, 0)
        gather_words(1, 0)
        quantize_w1(1, 0, 0, P)
        gather_words(1, 1)
        quantize_w1(1, 0, P, PASS)

        h, neg_top, bounded, linear, nudged, quiet, lesser = {}, {}, {}, {}, {}, {}, {}
        last = 2 * PACK - 1
        y_rows = [keep.tile([P, PACK, M], BF16, name="y_rows_%d" % b, align_bytes=64) for b in range(2)]
        woven = [keep.tile([P, M * PACK], BF16, name="woven_%d" % b, align_bytes=64) for b in range(2)]
        y_codes, y_sc, scores = {}, {}, {}

        def products(i):
            b, t = divmod(i, PACK)
            h[i] = ring.tile([P, S], F32, name="h")
            for half in range(2):
                bounded[i, half] = psum.tile([P, BANK], F32, name="acc")
                linear[i, half] = psum.tile([P, BANK], F32, name="acc")
            for a in range(2):
                for half in range(2):
                    cols = slice(half * BANK, (half + 1) * BANK)
                    wcols = slice(a * H + i * P, a * H + (i + 1) * P)
                    nc.tensor.matmul_mx(
                        out=bounded[i, half][:],
                        lhsT=w1_codes[a, b][:, t * P : (t + 1) * P].bitcast(FP8X4),
                        lhsT_scale=w1_sc[a, b][:, t * P : (t + 1) * P],
                        rhs=v_w[a, half][:].bitcast(FP8X4),
                        rhs_scale=v_sc[4 * a : P, cols],
                        start=(a == 0), stop=(a == 1),
                    )
                    nc.tensor.matmul_mx(
                        out=linear[i, half][:],
                        lhsT=w2_w[:, wcols].bitcast(FP4X4),
                        lhsT_scale=w2_sc[:, wcols],
                        rhs=v_w[a, half][:].bitcast(FP8X4),
                        rhs_scale=(v_sc, v_sc1)[a][:, cols],
                        start=(a == 0), stop=(a == 1),
                    )

        def bound(i, half):
            nc.scalar.activation(out=h[i][:, half * BANK : (half + 1) * BANK], in_=bounded[i, half][:], func=ACT.Tanh)

        def add_linear(i, half):
            cols = slice(half * BANK, (half + 1) * BANK)
            nc.vector.tensor_tensor(out=h[i][:, cols], in0=h[i][:, cols], in1=linear[i, half][:], op=ALU.add)

        def row_top(i):
            neg_top[i] = ring.tile([P, 1], F32, name="neg_top")
            nc.vector.tensor_reduce(out=neg_top[i][:], in_=h[i][:], axis=AXIS.X, op=ALU.max, negate=True)

        def look(i, lo, hi):
            lists = slice(lo // 16, hi // 16)
            nudged[i, lo] = ring.tile([P, hi - lo], F32, name="nudged")
            quiet[i, lo] = ring.tile([P, hi - lo], F32, name="quiet")
            nc.scalar.activation(
                out=nudged[i, lo][:], in_=h[i][:].indirect(pos1_sb[:, lists]), func=ACT.Exp,
                bias=rows["shift"][:, i : i + 1], scale=rows["temp"][:, i : i + 1],
            )
            nc.scalar.activation(
                out=quiet[i, lo][:], in_=h[i][:].indirect(pos2_sb[:, lists]), func=ACT.Exp, bias=neg_top[i][:],
            )

        def take_lesser(i, lo, hi):
            lesser[i, lo] = ring.tile([P, hi - lo], F32, name="lesser")
            nc.vector.scalar_tensor_tensor(
                out=lesser[i, lo][:], in0=nudged[i, lo][:], scalar=rows["lean"][:, i : i + 1], in1=quiet[i, lo][:],
                op0=ALU.mult, op1=ALU.min,
            )

        def apply_gain(i, lo, hi):
            b, t = divmod(i, PACK)
            nc.vector.tensor_scalar(
                out=y_rows[b][:, t, lo:hi], in0=lesser[i, lo][:], scalar1=rows["gain"][:, i : i + 1], scalar2=None,
                op0=ALU.mult,
            )

        def weave(b, lo, hi):
            nc.vector.tensor_copy(
                woven[b][:, PACK * lo : PACK * hi].rearrange("p (c i t) -> p c t i", i=4, t=PACK),
                y_rows[b][:, :, lo:hi].rearrange("p t (c i) -> p c t i", i=4),
            )

        def quantize_y(b, lo, hi):
            nc.vector.quantize_mx(
                out=y_codes[b][:, lo:hi].bitcast(FP8X4), scales=y_sc[b][:, lo:hi], in_=woven[b][:, PACK * lo : PACK * hi],
            )

        for b in range(2):
            y_codes[b] = keep.tile([P, M], U32, name="y_codes_%d" % b, align_bytes=64)
            y_sc[b] = keep.tile([P, M], U8, name="y_sc_%d" % b, align_bytes=64)

        def second_stage(b, half):
            cols = slice(half * HALF, (half + 1) * HALF)
            for pair in range(2):
                if b == 0:
                    scores[half, pair] = psum.tile([P, BANK], F32, name="acc")
                for u in range(2):
                    n0 = b * N + (2 * pair + u) * P
                    nc.tensor.matmul_mx(
                        out=scores[half, pair][:, u * HALF : (u + 1) * HALF],
                        lhsT=w3_w[:, n0 : n0 + P].bitcast(FP8X4),
                        lhsT_scale=w3_sc[:, n0 : n0 + P],
                        rhs=y_codes[b][:, cols].bitcast(FP8X4),
                        rhs_scale=y_sc[b][:, cols],
                        start=(b == 0 and u == 0), stop=(b == 1 and u == 1),
                    )

        def finish(half):
            for pair in range(2):
                result = keep.tile([P, BANK], F32, name="result_%d_%d" % (half, pair))
                nc.scalar.activation(out=result[:], in_=scores[half, pair][:], func=ACT.Tanh)
                (nc.scalar if half + pair == 2 else nc.sync).dma_start(
                    out[2 * pair * P : (2 * pair + 2) * P, half * HALF : (half + 1) * HALF].rearrange("(u p) m -> p u m", u=2),
                    result[:].rearrange("p (u m) -> p u m", u=2),
                )

        products(0)
        for half in range(2):
            bound(0, half)
            add_linear(0, half)
        row_top(0)
        for i in range(last):
            products(i + 1)
            if i > 0:
                take_lesser(i - 1, 0, M)
            for half in range(2):
                bound(i + 1, half)
                add_linear(i + 1, half)
            if i > 0:
                apply_gain(i - 1, 0, M)
            row_top(i + 1)
            look(i, 0, M)
            if i in (1, 2):
                quantize_w1(i - 1, 1)
            if i in (0, 1):
                round_w1(i, 1, nc.vector.tensor_copy)
            if i == PACK:
                weave(0, 0, M)
            if i == PACK + 1:
                quantize_y(0, 0, M)
        second_stage(0, 0)
        second_stage(0, 1)
        take_lesser(last - 1, 0, M)
        apply_gain(last - 1, 0, M)
        look(last, 0, HALF)
        look(last, HALF, M)
        take_lesser(last, 0, HALF)
        apply_gain(last, 0, HALF)
        weave(1, 0, HALF)
        take_lesser(last, HALF, M)
        quantize_y(1, 0, HALF)
        apply_gain(last, HALF, M)
        weave(1, HALF, M)
        quantize_y(1, HALF, M)
        for half in range(2):
            second_stage(1, half)
        for half in range(2):
            finish(half)
